import numpy as np
import ml_dtypes


def mxq(x, axis, fmt="e4m3"):
    dtype, down = {"e4m3": (ml_dtypes.float8_e4m3fn, 7), "e5m2": (ml_dtypes.float8_e5m2, 14)}[fmt]
    v = np.moveaxis(np.asarray(x, np.float32).astype(ml_dtypes.bfloat16).astype(np.float64), axis, -1)
    blocks = v.reshape(v.shape[:-1] + (-1, 32))
    amax = np.abs(blocks).max(-1, keepdims=True)
    byte = np.maximum(np.where(amax > 0, np.frexp(amax)[1] - 1 + 127, 0) - down, 1)
    scale = np.exp2(byte - 127.0)
    codes = (blocks / scale).astype(np.float32).astype(dtype).astype(np.float64)
    return np.moveaxis((codes * scale).reshape(v.shape), -1, axis)


WIDE = False


def mx_kscale(k):
    if not WIDE:
        return np.ones(k)
    levels = np.array([30, -30])
    if k % 512:
        return np.exp2(np.random.permutation(np.resize(levels, k // 32))).repeat(32)
    a = np.empty((k // 512, 16))
    for p in range(k // 512):
        a[p, :8] = np.random.permutation(np.resize(levels, 8))
        for g in range(8):
            far = levels[np.abs(levels - a[p, g]) >= 10]
            a[p, g + 8] = far[np.random.randint(len(far))]
    return np.exp2(a.ravel()).repeat(32)


BF16 = ml_dtypes.bfloat16


def bf(x):
    return np.asarray(x, np.float32).astype(BF16)


def f64(x):
    return np.asarray(x).astype(np.float64)


E2M1 = np.array([0.0, 0.5, 1.0, 1.5, 2.0, 3.0, 4.0, 6.0, -0.0, -0.5, -1.0, -1.5, -2.0, -3.0, -4.0, -6.0])


def pack_weight(w, fmt):
    k, n = w.shape
    w = f64(bf(w)).reshape(k // 32, 32, n)
    amax = np.abs(w).max(1)
    if fmt == "e4m3":
        byte = np.frexp(amax)[1] - 1 + 127 - 7
    else:
        mant, ex = np.frexp(amax / 6.0)
        byte = np.where(mant > 0.5, ex, ex - 1) + 127
    byte = np.clip(np.where(amax > 0, byte, 1), 1, 254)
    scaled = (w * np.exp2(127.0 - byte)[:, None, :]).reshape(k, n).astype(np.float32)
    by_word = np.ascontiguousarray(scaled.reshape(k // 512, 128, 4, n).transpose(0, 1, 3, 2))
    if fmt == "e4m3":
        words = by_word.astype(ml_dtypes.float8_e4m3fn).view(np.uint8)
    else:
        c = by_word.astype(ml_dtypes.float4_e2m1fn).view(np.uint8) & 0xF
        words = c[..., 0::2] | (c[..., 1::2] << 4)
    return np.ascontiguousarray(words), np.ascontiguousarray(byte.astype(np.uint8).reshape(k // 512, 16, n))


def unpack_weight(words, scales, fmt):
    g, p, n, _ = words.shape
    if fmt == "e4m3":
        vals = np.ascontiguousarray(words).view(ml_dtypes.float8_e4m3fn).astype(np.float64)
    else:
        nib = np.empty((g, p, n, 4), np.uint8)
        nib[..., 0::2] = words & 0xF
        nib[..., 1::2] = words >> 4
        vals = E2M1[nib]
    vals = vals * np.repeat(np.exp2(scales.astype(np.float64) - 127.0), 8, axis=1)[..., None]
    return vals.transpose(0, 1, 3, 2).reshape(g * 512, n)
def pack4(w):
    words, scales = pack_weight(w, "e2m1")
    return words.reshape(words.shape[0], 128, -1), scales


def unpack4(words, scales):
    return unpack_weight(words.reshape(words.shape[0], 128, -1, 2), scales, "e2m1")


M, K, N, F = 1024, 1024, 2048, 1024

SHARPNESS = 15.0


def setup_inputs():
    s, t = mx_kscale(K), mx_kscale(N)
    rca = 2.0 * np.random.standard_normal((M, K))
    row_c = np.random.uniform(0.5, 1.0, (K, 1))
    col_c = np.random.uniform(0.5, 1.0, (1, N))
    phi = row_c * col_c * np.random.uniform(0.0, 1.0, (K, N)) ** SHARPNESS
    phi_words, phi_scales = pack4(phi / s[:, None] * t)
    return {"rca": bf(rca * s),
            "phi_words": phi_words,
            "phi_scales": phi_scales,
            "totals": bf(phi.sum(axis=0)),
            "openness": bf(np.random.uniform(0.0, 1.0, (M, N))),
            "loadings": bf(3.0 * np.random.standard_normal((N, F)) / np.sqrt(N) / t[:, None]),
            "base": bf(0.2 * np.random.standard_normal(F))}


def reference(rca, phi_words, phi_scales, totals, openness, loadings, base):
    near = mxq(f64(rca), 1, "e4m3") @ unpack4(phi_words, phi_scales)
    density = near / f64(totals)
    chance = density * f64(openness)
    outlook = mxq(chance, 1, "e5m2") @ mxq(f64(loadings), 0, "e4m3")
    return outlook + f64(base)

@@ -1,0 +1,257 @@
+from contextlib import ExitStack
+
+import concourse.mybir as mybir
+from concourse.masks import make_identity
+
+M, K, N, F = 1024, 1024, 2048, 1024
+FLOPS = 2 * M * K * N + 2 * M * N * F
+
+F32 = mybir.dt.float32
+BF16 = mybir.dt.bfloat16
+I32 = mybir.dt.int32
+U32 = mybir.dt.uint32
+U8 = mybir.dt.uint8
+E4M3 = mybir.dt.float8_e4m3fn_x4
+E5M2 = mybir.dt.float8_e5m2_x4
+E2M1 = mybir.dt.float4_e2m1fn_x4
+COPY = mybir.ActivationFunctionType.Copy
+ALU = mybir.AluOpType
+
+P = 128
+W = 512
+
+
+def tile_product_space_density_s9_kernel(tc, rca, phi_words, phi_scales, totals, openness, loadings, base, out):
+    nc = tc.nc
+    with ExitStack() as ctx:
+        keep = ctx.enter_context(tc.tile_pool(name="keep", bufs=1))
+        stage = ctx.enter_context(tc.tile_pool(name="stage", bufs=2))
+        psum = ctx.enter_context(tc.psum_pool(name="psum", bufs=1))
+        ctx.enter_context(tc.manual_schedule())
+
+        def kept(name, shape, dtype):
+            return keep.tile(shape, dtype, name=name, align_bytes=256)
+
+        def bank(b):
+            return psum.tile([P, W], F32, name="bank%d" % b)
+
+        rca_raw = {(h, g): kept("rca_raw%d%d" % (h, g), [P, 4, W], BF16) for h in range(2) for g in range(2)}
+        open_raw = {(h, n): kept("open_raw%d%d" % (h, n), [P, 4, W], BF16) for h in range(2) for n in range(4)}
+        load_raw = {(n, f): kept("load_raw%d%d" % (n, f), [P, 4, W], BF16) for n in range(4) for f in range(2)}
+        phi_first = kept("phi_first", [P, 2, 2 * W], U8)
+        phi_rest = kept("phi_rest", [P, 2, 6 * W], U8)
+        sc_first = kept("sc_first", [P, 2, W], U8)
+        sc_rest = kept("sc_rest", [P, 2, 3 * W], U8)
+        phi_codes = [kept("phi_codes%d" % n, [P, 2, 4, 2 * P], U8) for n in range(4)]
+        phi_sc = [kept("phi_sc%d" % n, [P, 2, 4, P], U8) for n in range(4)]
+        rca_codes = {k: kept("rca_codes%d%d" % k, [P, W], U32) for k in rca_raw}
+        rca_sc = {k: kept("rca_sc%d%d" % k, [P, W], U8) for k in rca_raw}
+        ch_codes = {k: kept("ch_codes%d%d" % k, [P, W], U32) for k in open_raw}
+        ch_sc = {k: kept("ch_sc%d%d" % k, [P, W], U8) for k in open_raw}
+        ld_codes = {k: kept("ld_codes%d%d" % k, [P, W], U32) for k in load_raw}
+        ld_sc = {k: kept("ld_sc%d%d" % k, [P, W], U8) for k in load_raw}
+        tot = kept("tot", [P, 4, 4], BF16)
+        inv = kept("inv", [P, 4, 4], F32)
+        base_rows = kept("base_rows", [P, F], BF16)
+        ident = kept("ident", [P, P], F32)
+        warm_in = kept("warm_in", [P, 1], F32)
+        warm_out = kept("warm_out", [P, 1], F32)
+
+        words32 = phi_words.bitcast(I32)
+        scales32 = phi_scales.bitcast(I32)
+
+        def load_rows(dst, src, h, c):
+            nc.sync.dma_start(out=dst[:], in_=src[h * W:(h + 1) * W, c * W:(c + 1) * W].rearrange("(j p) k -> p j k", p=P))
+
+        def load_loadings(n, f):
+            nc.sync.dma_start(out=load_raw[n, f][:], in_=loadings[n * W:(n + 1) * W, f * W:(f + 1) * W].rearrange("(p t) f -> p t f", t=4))
+
+        def load_scales(dst, w0, w1):
+            for r in range(4):
+                nc.sync.dma_start(out=dst[r:P:32, :, :].bitcast(I32), in_=scales32[:, r:16:4, w0:w1].rearrange("g q w -> q g w"))
+
+        nc.vector.memset(sc_first[:].bitcast(I32), 0)
+        nc.vector.memset(warm_in[:], 0.0)
+        nc.vector.memset(sc_rest[:].bitcast(I32), 0)
+        make_identity(nc, ident[:])
+        nc.scalar.activation(out=warm_out[:], in_=warm_in[:], func=COPY, scale=warm_in[:])
+
+        load_rows(rca_raw[0, 0], rca, 0, 0)
+        nc.sync.dma_start(out=phi_first[:].bitcast(I32), in_=words32[:, :, 0:256].rearrange("g p w -> p g w"))
+        load_scales(sc_first, 0, 128)
+        load_rows(rca_raw[0, 1], rca, 0, 1)
+        nc.sync.dma_start(out=tot[:], in_=totals.rearrange("(n p t) -> p n t", p=P, t=4))
+        load_rows(open_raw[0, 0], openness, 0, 0)
+        nc.sync.dma_start(out=phi_rest[:].bitcast(I32), in_=words32[:, :, 256:1024].rearrange("g p w -> p g w"))
+        load_scales(sc_rest, 128, 512)
+        load_loadings(0, 0)
+        load_rows(open_raw[0, 1], openness, 0, 1)
+        load_rows(rca_raw[1, 0], rca, 1, 0)
+        load_loadings(1, 0)
+        load_rows(rca_raw[1, 1], rca, 1, 1)
+        load_rows(open_raw[0, 2], openness, 0, 2)
+        load_rows(open_raw[0, 3], openness, 0, 3)
+        load_loadings(2, 0)
+        load_rows(open_raw[1, 0], openness, 1, 0)
+        load_loadings(3, 0)
+        load_rows(open_raw[1, 1], openness, 1, 1)
+        load_rows(open_raw[1, 2], openness, 1, 2)
+        load_loadings(0, 1)
+        load_rows(open_raw[1, 3], openness, 1, 3)
+        nc.sync.dma_start(out=base_rows[:], in_=base.partition_broadcast(P))
+        load_loadings(1, 1)
+        load_loadings(2, 1)
+        load_loadings(3, 1)
+
+        rca_grouped = {}
+        ld_grouped = {}
+        ch_grouped = {}
+
+        def turn_rca(h, g, banks):
+            grouped = stage.tile([P, W, 4], BF16, name="rca_grouped", align_bytes=256)
+            rca_grouped[h, g] = grouped
+            for b in range(2):
+                acc = bank(banks[b])
+                view = acc[:].rearrange("p (u m) -> p u m", u=2)
+                for jj in range(2):
+                    words = rca_raw[h, g][:, 2 * b + jj, :].bitcast(F32)
+                    for u in range(2):
+                        nc.tensor.transpose(view[:, u, jj * P:(jj + 1) * P], words[:, u:256:2], ident[:])
+                nc.scalar.copy(out=grouped[:, 256 * b:256 * (b + 1), :].bitcast(F32), in_=view.rearrange("p u m -> p m u"))
+
+        def quantise(codes, scales, grouped, fmt):
+            nc.vector.quantize_mx(out=codes[:].bitcast(fmt), scales=scales[:], in_=grouped[:].rearrange("p m t -> p (m t)"))
+
+        def order_codes(n, g):
+            src = phi_first[:, g, :] if n == 0 else phi_rest[:, g, (n - 1) * 2 * W:n * 2 * W]
+            nc.vector.tensor_copy(out=phi_codes[n][:, g, :, :].rearrange("p t (m b) -> p t m b", b=2),
+                                  in_=src.rearrange("p (m t b) -> p t m b", t=4, b=2))
+
+        def order_scales(n):
+            src = sc_first[:, :, :] if n == 0 else sc_rest[:, :, (n - 1) * W:n * W]
+            nc.vector.tensor_copy(out=phi_sc[n][:], in_=src.rearrange("p g (m t) -> p g t m", t=4))
+
+        def first_pass(acc, h, n, t, g):
+            nc.tensor.matmul_mx(out=acc[:], lhsT=phi_codes[n][:, g, t, :].bitcast(E2M1), lhsT_scale=phi_sc[n][:, g, t, :],
+                                rhs=rca_codes[h, g][:].bitcast(E4M3), rhs_scale=rca_sc[h, g][:], start=(g == 0), stop=(g == 1))
+
+        def divide(density, acc, n, t):
+            nc.scalar.activation(out=density[:, t, :], in_=acc[:], func=COPY, scale=inv[:, n, t:t + 1])
+
+        def turn_openness(h, n, b, which):
+            acc = bank(which)
+            view = acc[:].rearrange("p (c u i) -> p c u i", u=2, i=2)
+            for jj in range(2):
+                words = open_raw[h, n][:, 2 * b + jj, :].bitcast(F32)
+                for u in range(2):
+                    nc.tensor.transpose(view[:, 64 * jj:64 * (jj + 1), u, :], words[:, u:256:2], ident[:])
+            return acc
+
+        def multiply(grouped, density, acc, b):
+            nc.vector.tensor_tensor(
+                out=grouped[:, 256 * b:256 * (b + 1), :].rearrange("p (c i) t -> p c t i", i=2),
+                in0=acc[:].bitcast(BF16).rearrange("p (w i e) -> p w e i", i=2, e=2),
+                in1=density[:, :, 256 * b:256 * (b + 1)].rearrange("p t (c i) -> p c t i", i=2),
+                op=ALU.mult)
+
+        def group_loadings(n, f, half):
+            if half == 0:
+                ld_grouped[n, f] = stage.tile([P, W, 4], BF16, name="ld_grouped", bufs=4, align_bytes=256)
+            cols = slice(256 * half, 256 * (half + 1))
+            nc.scalar.copy(out=ld_grouped[n, f][:, cols, :].rearrange("p (c i) t -> p c t i", i=4),
+                           in_=load_raw[n, f][:, :, cols].rearrange("p t (c i) -> p c t i", i=4))
+
+        def quantise_loadings(n, f):
+            quantise(ld_codes[n, f], ld_sc[n, f], ld_grouped[n, f], E4M3)
+
+        def quantise_chance(h, n):
+            quantise(ch_codes[h, n], ch_sc[h, n], ch_grouped[h, n], E5M2)
+
+        def second_pass(acc, mt, f, n):
+            h, cols = mt // 4, slice((mt % 4) * P, (mt % 4 + 1) * P)
+            nc.tensor.matmul_mx(out=acc[:], lhsT=ch_codes[h, n][:, cols].bitcast(E5M2), lhsT_scale=ch_sc[h, n][:, cols],
+                                rhs=ld_codes[n, f][:].bitcast(E4M3), rhs_scale=ld_sc[n, f][:], start=(n == 0), stop=(n == 3))
+
+        def finish(acc, mt, f):
+            result = stage.tile([P, W], F32, name="result", bufs=6)
+            nc.vector.tensor_tensor(out=result[:], in0=acc[:], in1=base_rows[:, f * W:(f + 1) * W], op=ALU.add)
+            nc.sync.dma_start(out=out[mt * P:(mt + 1) * P, f * W:(f + 1) * W], in_=result[:])
+
+        turn_rca(0, 0, [4, 5])
+        order_codes(0, 0)
+        order_scales(0)
+        quantise(rca_codes[0, 0], rca_sc[0, 0], rca_grouped[0, 0], E4M3)
+        order_codes(0, 1)
+        nc.vector.reciprocal(out=inv[:], in_=tot[:])
+        turn_rca(0, 1, [6, 7])
+        quantise(rca_codes[0, 1], rca_sc[0, 1], rca_grouped[0, 1], E4M3)
+
+        for step in range(8):
+            h, n = divmod(step, 4)
+            mine, other = ([4, 5], [6, 7]) if step % 2 == 0 else ([6, 7], [4, 5])
+            density = stage.tile([P, 4, W], F32, name="density", align_bytes=256)
+            if step == 0:
+                accs = [bank(t) for t in range(4)]
+                for t in range(4):
+                    first_pass(accs[t], h, n, t, 0)
+                for t in range(4):
+                    first_pass(accs[t], h, n, t, 1)
+                    divide(density, accs[t], n, t)
+                order_codes(1, 0)
+                order_codes(1, 1)
+                order_scales(1)
+            else:
+                for t in range(4):
+                    acc = bank(t)
+                    first_pass(acc, h, n, t, 0)
+                    first_pass(acc, h, n, t, 1)
+                    divide(density, acc, n, t)
+            turned = [turn_openness(h, n, b, mine[b]) for b in range(2)]
+            group_loadings(step // 2, 0, step % 2)
+            if step in (1, 2):
+                turn_rca(1, step - 1, other)
+            ch_grouped[h, n] = stage.tile([P, W, 4], BF16, name="ch_grouped", align_bytes=256)
+            multiply(ch_grouped[h, n], density, turned[0], 0)
+            if step > 0:
+                quantise_chance(*divmod(step - 1, 4))
+            if step < 2:
+                order_codes(step + 2, 0)
+            multiply(ch_grouped[h, n], density, turned[1], 1)
+            if step < 2:
+                order_codes(step + 2, 1)
+                order_scales(step + 2)
+            if step in (1, 2):
+                quantise(rca_codes[1, step - 1], rca_sc[1, step - 1], rca_grouped[1, step - 1], E4M3)
+            if step in (3, 4, 6, 7):
+                quantise_loadings([3, 4, 6, 7].index(step), 0)
+        quantise_chance(1, 3)
+
+        accs = [bank(mt) for mt in range(4)]
+        for n in range(4):
+            for mt in range(4):
+                second_pass(accs[mt], mt, 0, n)
+        for mt in range(8):
+            if mt % 2 == 0:
+                group_loadings(mt // 2, 1, 0)
+                group_loadings(mt // 2, 1, 1)
+            if mt < 4:
+                acc = accs[mt]
+            else:
+                acc = bank(mt)
+                for n in range(4):
+                    second_pass(acc, mt, 0, n)
+            finish(acc, mt, 0)
+            if mt in (1, 3, 5, 6):
+                quantise_loadings([1, 3, 5, 6].index(mt), 1)
+        accs = [bank(mt) for mt in range(2)]
+        for n in range(4):
+            for mt in range(2):
+                second_pass(accs[mt], mt, 1, n)
+        for mt in range(8):
+            if mt < 2:
+                acc = accs[mt]
+            else:
+                acc = bank(mt)
+                for n in range(4):
+                    second_pass(acc, mt, 1, n)
+            finish(acc, mt, 1)

@@ -38,8 +38,7 @@ def tile_product_space_density_s9_kernel(tc, rca, phi_words, phi_scales, totals,
         rca_raw = {(h, g): kept("rca_raw%d%d" % (h, g), [P, 4, W], BF16) for h in range(2) for g in range(2)}
         open_raw = {(h, n): kept("open_raw%d%d" % (h, n), [P, 4, W], BF16) for h in range(2) for n in range(4)}
         load_raw = {(n, f): kept("load_raw%d%d" % (n, f), [P, 4, W], BF16) for n in range(4) for f in range(2)}
-        phi_first = kept("phi_first", [P, 2, 2 * W], U8)
-        phi_rest = kept("phi_rest", [P, 2, 6 * W], U8)
+        phi_raw = [kept("phi_raw%d" % i, [P, 2, 2 * W * c], U8) for i, c in enumerate((1, 1, 2))]
         sc_first = kept("sc_first", [P, 2, W], U8)
         sc_rest = kept("sc_rest", [P, 2, 3 * W], U8)
         phi_codes = [kept("phi_codes%d" % n, [P, 2, 4, 2 * P], U8) for n in range(4)]
@@ -77,19 +76,22 @@ def tile_product_space_density_s9_kernel(tc, rca, phi_words, phi_scales, totals,
         nc.scalar.activation(out=warm_out[:], in_=warm_in[:], func=COPY, scale=warm_in[:])
 
         load_rows(rca_raw[0, 0], rca, 0, 0)
-        nc.sync.dma_start(out=phi_first[:].bitcast(I32), in_=words32[:, :, 0:256].rearrange("g p w -> p g w"))
+        nc.sync.dma_start(out=phi_raw[0][:].bitcast(I32), in_=words32[:, :, 0:256].rearrange("g p w -> p g w"))
         load_scales(sc_first, 0, 128)
-        load_rows(rca_raw[0, 1], rca, 0, 1)
+        for b in range(2):
+            nc.sync.dma_start(out=rca_raw[0, 1][:, 2 * b:2 * b + 2, :],
+                              in_=rca[256 * b:256 * (b + 1), W:2 * W].rearrange("(j p) k -> p j k", p=P))
         nc.sync.dma_start(out=tot[:], in_=totals.rearrange("(n p t) -> p n t", p=P, t=4))
-        load_rows(open_raw[0, 0], openness, 0, 0)
-        nc.sync.dma_start(out=phi_rest[:].bitcast(I32), in_=words32[:, :, 256:1024].rearrange("g p w -> p g w"))
-        load_scales(sc_rest, 128, 512)
         load_loadings(0, 0)
+        nc.sync.dma_start(out=phi_raw[1][:].bitcast(I32), in_=words32[:, :, 256:512].rearrange("g p w -> p g w"))
+        load_scales(sc_rest, 128, 512)
+        load_rows(open_raw[0, 0], openness, 0, 0)
+        nc.sync.dma_start(out=phi_raw[2][:].bitcast(I32), in_=words32[:, :, 512:1024].rearrange("g p w -> p g w"))
         load_rows(open_raw[0, 1], openness, 0, 1)
         load_rows(rca_raw[1, 0], rca, 1, 0)
         load_loadings(1, 0)
-        load_rows(rca_raw[1, 1], rca, 1, 1)
         load_rows(open_raw[0, 2], openness, 0, 2)
+        load_rows(rca_raw[1, 1], rca, 1, 1)
         load_rows(open_raw[0, 3], openness, 0, 3)
         load_loadings(2, 0)
         load_rows(open_raw[1, 0], openness, 1, 0)
@@ -107,7 +109,7 @@ def tile_product_space_density_s9_kernel(tc, rca, phi_words, phi_scales, totals,
         ld_grouped = {}
         ch_grouped = {}
 
-        def turn_rca(h, g, banks):
+        def turn_rca(h, g, banks, split=False):
             grouped = stage.tile([P, W, 4], BF16, name="rca_grouped", align_bytes=256)
             rca_grouped[h, g] = grouped
             for b in range(2):
@@ -117,15 +119,20 @@ def tile_product_space_density_s9_kernel(tc, rca, phi_words, phi_scales, totals,
                     words = rca_raw[h, g][:, 2 * b + jj, :].bitcast(F32)
                     for u in range(2):
                         nc.tensor.transpose(view[:, u, jj * P:(jj + 1) * P], words[:, u:256:2], ident[:])
-                nc.scalar.copy(out=grouped[:, 256 * b:256 * (b + 1), :].bitcast(F32), in_=view.rearrange("p u m -> p m u"))
+                copy = nc.vector.tensor_copy if split and b == 1 else nc.scalar.copy
+                copy(out=grouped[:, 256 * b:256 * (b + 1), :].bitcast(F32), in_=view.rearrange("p u m -> p m u"))
 
         def quantise(codes, scales, grouped, fmt):
             nc.vector.quantize_mx(out=codes[:].bitcast(fmt), scales=scales[:], in_=grouped[:].rearrange("p m t -> p (m t)"))
 
         def order_codes(n, g):
-            src = phi_first[:, g, :] if n == 0 else phi_rest[:, g, (n - 1) * 2 * W:n * 2 * W]
             nc.vector.tensor_copy(out=phi_codes[n][:, g, :, :].rearrange("p t (m b) -> p t m b", b=2),
-                                  in_=src.rearrange("p (m t b) -> p t m b", t=4, b=2))
+                                  in_=phi_raw[n][:, g, :].rearrange("p (m t b) -> p t m b", t=4, b=2))
+
+        def order_both(n):
+            src = phi_raw[1][:, :, :] if n == 1 else phi_raw[2][:, :, (n - 2) * 2 * W:(n - 1) * 2 * W]
+            nc.vector.tensor_copy(out=phi_codes[n][:].rearrange("p g t (m b) -> p g t m b", b=2),
+                                  in_=src.rearrange("p g (m t b) -> p g t m b", t=4, b=2))
 
         def order_scales(n):
             src = sc_first[:, :, :] if n == 0 else sc_rest[:, :, (n - 1) * W:n * W]
@@ -154,12 +161,12 @@ def tile_product_space_density_s9_kernel(tc, rca, phi_words, phi_scales, totals,
                 in1=density[:, :, 256 * b:256 * (b + 1)].rearrange("p t (c i) -> p c t i", i=2),
                 op=ALU.mult)
 
-        def group_loadings(n, f, half):
+        def group_loadings(n, f, half, copy=nc.scalar.copy):
             if half == 0:
                 ld_grouped[n, f] = stage.tile([P, W, 4], BF16, name="ld_grouped", bufs=4, align_bytes=256)
             cols = slice(256 * half, 256 * (half + 1))
-            nc.scalar.copy(out=ld_grouped[n, f][:, cols, :].rearrange("p (c i) t -> p c t i", i=4),
-                           in_=load_raw[n, f][:, :, cols].rearrange("p t (c i) -> p c t i", i=4))
+            copy(out=ld_grouped[n, f][:, cols, :].rearrange("p (c i) t -> p c t i", i=4),
+                 in_=load_raw[n, f][:, :, cols].rearrange("p t (c i) -> p c t i", i=4))
 
         def quantise_loadings(n, f):
             quantise(ld_codes[n, f], ld_sc[n, f], ld_grouped[n, f], E4M3)
@@ -172,86 +179,162 @@ def tile_product_space_density_s9_kernel(tc, rca, phi_words, phi_scales, totals,
             nc.tensor.matmul_mx(out=acc[:], lhsT=ch_codes[h, n][:, cols].bitcast(E5M2), lhsT_scale=ch_sc[h, n][:, cols],
                                 rhs=ld_codes[n, f][:].bitcast(E4M3), rhs_scale=ld_sc[n, f][:], start=(n == 0), stop=(n == 3))
 
-        def finish(acc, mt, f):
+        def finish(mt, f, pieces=1):
             result = stage.tile([P, W], F32, name="result", bufs=6)
-            nc.vector.tensor_tensor(out=result[:], in0=acc[:], in1=base_rows[:, f * W:(f + 1) * W], op=ALU.add)
-            nc.sync.dma_start(out=out[mt * P:(mt + 1) * P, f * W:(f + 1) * W], in_=result[:])
+            width = W // pieces
+            for c in range(0, W, width):
+                nc.vector.tensor_tensor(out=result[:, c:c + width], in0=sums[mt][:, c:c + width],
+                                        in1=base_rows[:, f * W + c:f * W + c + width], op=ALU.add)
+                nc.sync.dma_start(out=out[mt * P:(mt + 1) * P, f * W + c:f * W + c + width], in_=result[:, c:c + width])
 
-        turn_rca(0, 0, [4, 5])
-        order_codes(0, 0)
-        order_scales(0)
-        quantise(rca_codes[0, 0], rca_sc[0, 0], rca_grouped[0, 0], E4M3)
-        order_codes(0, 1)
-        nc.vector.reciprocal(out=inv[:], in_=tot[:])
-        turn_rca(0, 1, [6, 7])
-        quantise(rca_codes[0, 1], rca_sc[0, 1], rca_grouped[0, 1], E4M3)
+        density = {}
+        turned = {}
+        sums = {}
 
-        for step in range(8):
+        def quantise_rca(h, g):
+            quantise(rca_codes[h, g], rca_sc[h, g], rca_grouped[h, g], E4M3)
+
+        def near(step):
             h, n = divmod(step, 4)
-            mine, other = ([4, 5], [6, 7]) if step % 2 == 0 else ([6, 7], [4, 5])
-            density = stage.tile([P, 4, W], F32, name="density", align_bytes=256)
+            density[step] = stage.tile([P, 4, W], F32, name="density", align_bytes=256)
             if step == 0:
                 accs = [bank(t) for t in range(4)]
                 for t in range(4):
                     first_pass(accs[t], h, n, t, 0)
                 for t in range(4):
                     first_pass(accs[t], h, n, t, 1)
-                    divide(density, accs[t], n, t)
-                order_codes(1, 0)
-                order_codes(1, 1)
-                order_scales(1)
+                    divide(density[step], accs[t], n, t)
             else:
                 for t in range(4):
                     acc = bank(t)
                     first_pass(acc, h, n, t, 0)
                     first_pass(acc, h, n, t, 1)
-                    divide(density, acc, n, t)
-            turned = [turn_openness(h, n, b, mine[b]) for b in range(2)]
-            group_loadings(step // 2, 0, step % 2)
-            if step in (1, 2):
-                turn_rca(1, step - 1, other)
-            ch_grouped[h, n] = stage.tile([P, W, 4], BF16, name="ch_grouped", align_bytes=256)
-            multiply(ch_grouped[h, n], density, turned[0], 0)
-            if step > 0:
-                quantise_chance(*divmod(step - 1, 4))
-            if step < 2:
-                order_codes(step + 2, 0)
-            multiply(ch_grouped[h, n], density, turned[1], 1)
-            if step < 2:
-                order_codes(step + 2, 1)
-                order_scales(step + 2)
-            if step in (1, 2):
-                quantise(rca_codes[1, step - 1], rca_sc[1, step - 1], rca_grouped[1, step - 1], E4M3)
-            if step in (3, 4, 6, 7):
-                quantise_loadings([3, 4, 6, 7].index(step), 0)
-        quantise_chance(1, 3)
+                    divide(density[step], acc, n, t)
 
-        accs = [bank(mt) for mt in range(4)]
-        for n in range(4):
-            for mt in range(4):
-                second_pass(accs[mt], mt, 0, n)
-        for mt in range(8):
-            if mt % 2 == 0:
-                group_loadings(mt // 2, 1, 0)
-                group_loadings(mt // 2, 1, 1)
-            if mt < 4:
-                acc = accs[mt]
-            else:
-                acc = bank(mt)
-                for n in range(4):
-                    second_pass(acc, mt, 0, n)
-            finish(acc, mt, 0)
-            if mt in (1, 3, 5, 6):
-                quantise_loadings([1, 3, 5, 6].index(mt), 1)
-        accs = [bank(mt) for mt in range(2)]
-        for n in range(4):
-            for mt in range(2):
-                second_pass(accs[mt], mt, 1, n)
-        for mt in range(8):
-            if mt < 2:
-                acc = accs[mt]
-            else:
-                acc = bank(mt)
-                for n in range(4):
-                    second_pass(acc, mt, 1, n)
-            finish(acc, mt, 1)
+        def turn(step):
+            h, n = divmod(step, 4)
+            turned[step] = [turn_openness(h, n, b, 4 + 2 * (step % 2) + b) for b in range(2)]
+
+        def mul(step, b):
+            if b == 0:
+                ch_grouped[divmod(step, 4)] = stage.tile([P, W, 4], BF16, name="ch_grouped", align_bytes=256)
+            multiply(ch_grouped[divmod(step, 4)], density[step], turned[step][b], b)
+
+        def qc(step):
+            quantise_chance(*divmod(step, 4))
+
+        def second(f, first, count):
+            for mt in range(first, first + count):
+                sums[mt] = bank(mt)
+            for n in range(4):
+                for mt in range(first, first + count):
+                    second_pass(sums[mt], mt, f, n)
+
+        turn_rca(0, 0, [4, 5])
+        order_codes(0, 0)
+        order_scales(0)
+        quantise_rca(0, 0)
+        order_codes(0, 1)
+        turn_rca(0, 1, [6, 7], split=True)
+        quantise_rca(0, 1)
+        nc.vector.reciprocal(out=inv[:], in_=tot[:])
+        group_loadings(0, 0, 0)
+        group_loadings(0, 0, 1)
+        near(0)
+        order_both(1)
+        order_scales(1)
+        order_scales(2)
+        order_scales(3)
+        turn(0)
+        mul(0, 0)
+        order_both(2)
+        mul(0, 1)
+        near(1)
+        turn(1)
+        group_loadings(1, 0, 0)
+        turn_rca(1, 0, [4, 5])
+        mul(1, 0)
+        qc(0)
+        mul(1, 1)
+        order_both(3)
+        near(2)
+        turn(2)
+        group_loadings(1, 0, 1)
+        turn_rca(1, 1, [6, 7])
+        quantise_rca(1, 0)
+        mul(2, 0)
+        qc(1)
+        mul(2, 1)
+        quantise_loadings(0, 0)
+        near(3)
+        turn(3)
+        group_loadings(2, 0, 0)
+        quantise_rca(1, 1)
+        mul(3, 0)
+        qc(2)
+        mul(3, 1)
+        near(4)
+        turn(4)
+        group_loadings(2, 0, 1)
+        mul(4, 0)
+        qc(3)
+        mul(4, 1)
+        quantise_loadings(1, 0)
+        near(5)
+        turn(5)
+        group_loadings(3, 0, 0)
+        mul(5, 0)
+        qc(4)
+        mul(5, 1)
+        near(6)
+        turn(6)
+        group_loadings(3, 0, 1)
+        mul(6, 0)
+        qc(5)
+        mul(6, 1)
+        quantise_loadings(2, 0)
+        near(7)
+        turn(7)
+        group_loadings(0, 1, 0)
+        mul(7, 0)
+        qc(6)
+        quantise_loadings(3, 0)
+        mul(7, 1)
+        qc(7)
+        group_loadings(0, 1, 1)
+        second(0, 0, 5)
+        quantise_loadings(0, 1)
+        group_loadings(1, 1, 0)
+        group_loadings(1, 1, 1)
+        finish(0, 0)
+        finish(1, 0)
+        quantise_loadings(1, 1)
+        second(0, 5, 1)
+        finish(2, 0)
+        finish(3, 0)
+        group_loadings(2, 1, 0)
+        group_loadings(2, 1, 1)
+        second(0, 6, 1)
+        quantise_loadings(2, 1)
+        finish(4, 0)
+        second(0, 7, 1)
+        group_loadings(3, 1, 0)
+        group_loadings(3, 1, 1)
+        quantise_loadings(3, 1)
+        finish(5, 0)
+        finish(6, 0)
+        second(1, 0, 3)
+        finish(7, 0)
+        finish(0, 1)
+        finish(1, 1)
+        finish(2, 1)
+        second(1, 3, 1)
+        finish(3, 1)
+        second(1, 4, 1)
+        finish(4, 1)
+        second(1, 5, 1)
+        finish(5, 1)
+        second(1, 6, 1)
+        finish(6, 1)
+        second(1, 7, 1)
+        finish(7, 1, 2)

@@ -39,8 +39,8 @@ def tile_product_space_density_s9_kernel(tc, rca, phi_words, phi_scales, totals,
         open_raw = {(h, n): kept("open_raw%d%d" % (h, n), [P, 4, W], BF16) for h in range(2) for n in range(4)}
         load_raw = {(n, f): kept("load_raw%d%d" % (n, f), [P, 4, W], BF16) for n in range(4) for f in range(2)}
         phi_raw = [kept("phi_raw%d" % i, [P, 2, 2 * W * c], U8) for i, c in enumerate((1, 1, 2))]
-        sc_first = kept("sc_first", [P, 2, W], U8)
-        sc_rest = kept("sc_rest", [P, 2, 3 * W], U8)
+        sc_first = kept("sc_first", [P, 2, 2 * W], U8)
+        sc_rest = kept("sc_rest", [P, 2, 2 * W], U8)
         phi_codes = [kept("phi_codes%d" % n, [P, 2, 4, 2 * P], U8) for n in range(4)]
         phi_sc = [kept("phi_sc%d" % n, [P, 2, 4, P], U8) for n in range(4)]
         rca_codes = {k: kept("rca_codes%d%d" % k, [P, W], U32) for k in rca_raw}
@@ -77,19 +77,19 @@ def tile_product_space_density_s9_kernel(tc, rca, phi_words, phi_scales, totals,
 
         load_rows(rca_raw[0, 0], rca, 0, 0)
         nc.sync.dma_start(out=phi_raw[0][:].bitcast(I32), in_=words32[:, :, 0:256].rearrange("g p w -> p g w"))
-        load_scales(sc_first, 0, 128)
+        load_scales(sc_first, 0, 256)
         for b in range(2):
             nc.sync.dma_start(out=rca_raw[0, 1][:, 2 * b:2 * b + 2, :],
                               in_=rca[256 * b:256 * (b + 1), W:2 * W].rearrange("(j p) k -> p j k", p=P))
         nc.sync.dma_start(out=tot[:], in_=totals.rearrange("(n p t) -> p n t", p=P, t=4))
         load_loadings(0, 0)
         nc.sync.dma_start(out=phi_raw[1][:].bitcast(I32), in_=words32[:, :, 256:512].rearrange("g p w -> p g w"))
-        load_scales(sc_rest, 128, 512)
         load_rows(open_raw[0, 0], openness, 0, 0)
+        load_scales(sc_rest, 256, 512)
         nc.sync.dma_start(out=phi_raw[2][:].bitcast(I32), in_=words32[:, :, 512:1024].rearrange("g p w -> p g w"))
         load_rows(open_raw[0, 1], openness, 0, 1)
-        load_rows(rca_raw[1, 0], rca, 1, 0)
         load_loadings(1, 0)
+        load_rows(rca_raw[1, 0], rca, 1, 0)
         load_rows(open_raw[0, 2], openness, 0, 2)
         load_rows(rca_raw[1, 1], rca, 1, 1)
         load_rows(open_raw[0, 3], openness, 0, 3)
@@ -135,7 +135,7 @@ def tile_product_space_density_s9_kernel(tc, rca, phi_words, phi_scales, totals,
                                   in_=src.rearrange("p g (m t b) -> p g t m b", t=4, b=2))
 
         def order_scales(n):
-            src = sc_first[:, :, :] if n == 0 else sc_rest[:, :, (n - 1) * W:n * W]
+            src = (sc_first if n < 2 else sc_rest)[:, :, (n % 2) * W:(n % 2 + 1) * W]
             nc.vector.tensor_copy(out=phi_sc[n][:], in_=src.rearrange("p g (m t) -> p g t m", t=4))
 
         def first_pass(acc, h, n, t, g):
@@ -194,9 +194,10 @@ def tile_product_space_density_s9_kernel(tc, rca, phi_words, phi_scales, totals,
         def quantise_rca(h, g):
             quantise(rca_codes[h, g], rca_sc[h, g], rca_grouped[h, g], E4M3)
 
-        def near(step):
+        def near(step, slots=range(4)):
             h, n = divmod(step, 4)
-            density[step] = stage.tile([P, 4, W], F32, name="density", align_bytes=256)
+            if slots[0] == 0:
+                density[step] = stage.tile([P, 4, W], F32, name="density", align_bytes=256)
             if step == 0:
                 accs = [bank(t) for t in range(4)]
                 for t in range(4):
@@ -205,7 +206,7 @@ def tile_product_space_density_s9_kernel(tc, rca, phi_words, phi_scales, totals,
                     first_pass(accs[t], h, n, t, 1)
                     divide(density[step], accs[t], n, t)
             else:
-                for t in range(4):
+                for t in slots:
                     acc = bank(t)
                     first_pass(acc, h, n, t, 0)
                     first_pass(acc, h, n, t, 1)
@@ -239,10 +240,10 @@ def tile_product_space_density_s9_kernel(tc, rca, phi_words, phi_scales, totals,
         quantise_rca(0, 1)
         nc.vector.reciprocal(out=inv[:], in_=tot[:])
         group_loadings(0, 0, 0)
-        group_loadings(0, 0, 1)
         near(0)
-        order_both(1)
+        group_loadings(0, 0, 1)
         order_scales(1)
+        order_both(1)
         order_scales(2)
         order_scales(3)
         turn(0)
@@ -252,21 +253,23 @@ def tile_product_space_density_s9_kernel(tc, rca, phi_words, phi_scales, totals,
         near(1)
         turn(1)
         group_loadings(1, 0, 0)
-        turn_rca(1, 0, [4, 5])
         mul(1, 0)
+        order_both(3)
         qc(0)
         mul(1, 1)
-        order_both(3)
-        near(2)
+        near(2, (0, 1))
+        turn_rca(1, 0, [4, 5])
+        near(2, (2, 3))
         turn(2)
         group_loadings(1, 0, 1)
-        turn_rca(1, 1, [6, 7])
         quantise_rca(1, 0)
         mul(2, 0)
         qc(1)
         mul(2, 1)
         quantise_loadings(0, 0)
-        near(3)
+        near(3, (0, 1))
+        turn_rca(1, 1, [6, 7])
+        near(3, (2, 3))
         turn(3)
         group_loadings(2, 0, 0)
         quantise_rca(1, 1)

from contextlib import ExitStack

import concourse.mybir as mybir
from concourse.masks import make_identity

M, K, N, F = 1024, 1024, 2048, 1024
FLOPS = 2 * M * K * N + 2 * M * N * F

F32 = mybir.dt.float32
BF16 = mybir.dt.bfloat16
I32 = mybir.dt.int32
U32 = mybir.dt.uint32
U8 = mybir.dt.uint8
E4M3 = mybir.dt.float8_e4m3fn_x4
E5M2 = mybir.dt.float8_e5m2_x4
E2M1 = mybir.dt.float4_e2m1fn_x4
COPY = mybir.ActivationFunctionType.Copy
ALU = mybir.AluOpType

P = 128
W = 512


def tile_product_space_density_s9_kernel(tc, rca, phi_words, phi_scales, totals, openness, loadings, base, out):
    nc = tc.nc
    with ExitStack() as ctx:
        keep = ctx.enter_context(tc.tile_pool(name="keep", bufs=1))
        stage = ctx.enter_context(tc.tile_pool(name="stage", bufs=2))
        psum = ctx.enter_context(tc.psum_pool(name="psum", bufs=1))
        ctx.enter_context(tc.manual_schedule())

        def kept(name, shape, dtype):
            return keep.tile(shape, dtype, name=name, align_bytes=256)

        def bank(b):
            return psum.tile([P, W], F32, name="bank%d" % b)

        rca_raw = {(h, g): kept("rca_raw%d%d" % (h, g), [P, 4, W], BF16) for h in range(2) for g in range(2)}
        open_raw = {(h, n): kept("open_raw%d%d" % (h, n), [P, 4, W], BF16) for h in range(2) for n in range(4)}
        load_raw = {(n, f): kept("load_raw%d%d" % (n, f), [P, 4, W], BF16) for n in range(4) for f in range(2)}
        phi_raw = [kept("phi_raw%d" % i, [P, 2, 2 * W * c], U8) for i, c in enumerate((1, 1, 2))]
        sc_first = kept("sc_first", [P, 2, 2 * W], U8)
        sc_rest = kept("sc_rest", [P, 2, 2 * W], U8)
        phi_codes = [kept("phi_codes%d" % n, [P, 2, 4, 2 * P], U8) for n in range(4)]
        phi_sc = [kept("phi_sc%d" % n, [P, 2, 4, P], U8) for n in range(4)]
        rca_codes = {k: kept("rca_codes%d%d" % k, [P, W], U32) for k in rca_raw}
        rca_sc = {k: kept("rca_sc%d%d" % k, [P, W], U8) for k in rca_raw}
        ch_codes = {k: kept("ch_codes%d%d" % k, [P, W], U32) for k in open_raw}
        ch_sc = {k: kept("ch_sc%d%d" % k, [P, W], U8) for k in open_raw}
        ld_codes = {k: kept("ld_codes%d%d" % k, [P, W], U32) for k in load_raw}
        ld_sc = {k: kept("ld_sc%d%d" % k, [P, W], U8) for k in load_raw}
        tot = kept("tot", [P, 4, 4], BF16)
        inv = kept("inv", [P, 4, 4], F32)
        base_rows = kept("base_rows", [P, F], BF16)
        ident = kept("ident", [P, P], F32)
        warm_in = kept("warm_in", [P, 1], F32)
        warm_out = kept("warm_out", [P, 1], F32)

        words32 = phi_words.bitcast(I32)
        scales32 = phi_scales.bitcast(I32)

        def load_rows(dst, src, h, c):
            nc.sync.dma_start(out=dst[:], in_=src[h * W:(h + 1) * W, c * W:(c + 1) * W].rearrange("(j p) k -> p j k", p=P))

        def load_loadings(n, f):
            nc.sync.dma_start(out=load_raw[n, f][:], in_=loadings[n * W:(n + 1) * W, f * W:(f + 1) * W].rearrange("(p t) f -> p t f", t=4))

        def load_scales(dst, w0, w1):
            for r in range(4):
                nc.sync.dma_start(out=dst[r:P:32, :, :].bitcast(I32), in_=scales32[:, r:16:4, w0:w1].rearrange("g q w -> q g w"))

        nc.vector.memset(sc_first[:].bitcast(I32), 0)
        nc.vector.memset(warm_in[:], 0.0)
        nc.vector.memset(sc_rest[:].bitcast(I32), 0)
        make_identity(nc, ident[:])
        nc.scalar.activation(out=warm_out[:], in_=warm_in[:], func=COPY, scale=warm_in[:])

        load_rows(rca_raw[0, 0], rca, 0, 0)
        nc.sync.dma_start(out=phi_raw[0][:].bitcast(I32), in_=words32[:, :, 0:256].rearrange("g p w -> p g w"))
        load_scales(sc_first, 0, 256)
        for b in range(2):
            nc.sync.dma_start(out=rca_raw[0, 1][:, 2 * b:2 * b + 2, :],
                              in_=rca[256 * b:256 * (b + 1), W:2 * W].rearrange("(j p) k -> p j k", p=P))
        nc.sync.dma_start(out=tot[:], in_=totals.rearrange("(n p t) -> p n t", p=P, t=4))
        load_loadings(0, 0)
        nc.sync.dma_start(out=phi_raw[1][:].bitcast(I32), in_=words32[:, :, 256:512].rearrange("g p w -> p g w"))
        load_rows(open_raw[0, 0], openness, 0, 0)
        load_scales(sc_rest, 256, 512)
        nc.sync.dma_start(out=phi_raw[2][:].bitcast(I32), in_=words32[:, :, 512:1024].rearrange("g p w -> p g w"))
        load_rows(open_raw[0, 1], openness, 0, 1)
        load_loadings(1, 0)
        load_rows(rca_raw[1, 0], rca, 1, 0)
        load_rows(open_raw[0, 2], openness, 0, 2)
        load_rows(rca_raw[1, 1], rca, 1, 1)
        load_rows(open_raw[0, 3], openness, 0, 3)
        load_loadings(2, 0)
        load_rows(open_raw[1, 0], openness, 1, 0)
        load_loadings(3, 0)
        load_rows(open_raw[1, 1], openness, 1, 1)
        load_rows(open_raw[1, 2], openness, 1, 2)
        load_loadings(0, 1)
        load_rows(open_raw[1, 3], openness, 1, 3)
        nc.sync.dma_start(out=base_rows[:], in_=base.partition_broadcast(P))
        load_loadings(1, 1)
        load_loadings(2, 1)
        load_loadings(3, 1)

        rca_grouped = {}
        ld_grouped = {}
        ch_grouped = {}

        def turn_rca(h, g, banks, split=False):
            grouped = stage.tile([P, W, 4], BF16, name="rca_grouped", align_bytes=256)
            rca_grouped[h, g] = grouped
            for b in range(2):
                acc = bank(banks[b])
                view = acc[:].rearrange("p (u m) -> p u m", u=2)
                for jj in range(2):
                    words = rca_raw[h, g][:, 2 * b + jj, :].bitcast(F32)
                    for u in range(2):
                        nc.tensor.transpose(view[:, u, jj * P:(jj + 1) * P], words[:, u:256:2], ident[:])
                copy = nc.vector.tensor_copy if split and b == 1 else nc.scalar.copy
                copy(out=grouped[:, 256 * b:256 * (b + 1), :].bitcast(F32), in_=view.rearrange("p u m -> p m u"))

        def quantise(codes, scales, grouped, fmt):
            nc.vector.quantize_mx(out=codes[:].bitcast(fmt), scales=scales[:], in_=grouped[:].rearrange("p m t -> p (m t)"))

        def order_codes(n, g):
            nc.vector.tensor_copy(out=phi_codes[n][:, g, :, :].rearrange("p t (m b) -> p t m b", b=2),
                                  in_=phi_raw[n][:, g, :].rearrange("p (m t b) -> p t m b", t=4, b=2))

        def order_both(n):
            src = phi_raw[1][:, :, :] if n == 1 else phi_raw[2][:, :, (n - 2) * 2 * W:(n - 1) * 2 * W]
            nc.vector.tensor_copy(out=phi_codes[n][:].rearrange("p g t (m b) -> p g t m b", b=2),
                                  in_=src.rearrange("p g (m t b) -> p g t m b", t=4, b=2))

        def order_scales(n):
            src = (sc_first if n < 2 else sc_rest)[:, :, (n % 2) * W:(n % 2 + 1) * W]
            nc.vector.tensor_copy(out=phi_sc[n][:], in_=src.rearrange("p g (m t) -> p g t m", t=4))

        def first_pass(acc, h, n, t, g):
            nc.tensor.matmul_mx(out=acc[:], lhsT=phi_codes[n][:, g, t, :].bitcast(E2M1), lhsT_scale=phi_sc[n][:, g, t, :],
                                rhs=rca_codes[h, g][:].bitcast(E4M3), rhs_scale=rca_sc[h, g][:], start=(g == 0), stop=(g == 1))

        def divide(density, acc, n, t):
            nc.scalar.activation(out=density[:, t, :], in_=acc[:], func=COPY, scale=inv[:, n, t:t + 1])

        def turn_openness(h, n, b, which):
            acc = bank(which)
            view = acc[:].rearrange("p (c u i) -> p c u i", u=2, i=2)
            for jj in range(2):
                words = open_raw[h, n][:, 2 * b + jj, :].bitcast(F32)
                for u in range(2):
                    nc.tensor.transpose(view[:, 64 * jj:64 * (jj + 1), u, :], words[:, u:256:2], ident[:])
            return acc

        def multiply(grouped, density, acc, b):
            nc.vector.tensor_tensor(
                out=grouped[:, 256 * b:256 * (b + 1), :].rearrange("p (c i) t -> p c t i", i=2),
                in0=acc[:].bitcast(BF16).rearrange("p (w i e) -> p w e i", i=2, e=2),
                in1=density[:, :, 256 * b:256 * (b + 1)].rearrange("p t (c i) -> p c t i", i=2),
                op=ALU.mult)

        def group_loadings(n, f, half, copy=nc.scalar.copy):
            if half == 0:
                ld_grouped[n, f] = stage.tile([P, W, 4], BF16, name="ld_grouped", bufs=4, align_bytes=256)
            cols = slice(256 * half, 256 * (half + 1))
            copy(out=ld_grouped[n, f][:, cols, :].rearrange("p (c i) t -> p c t i", i=4),
                 in_=load_raw[n, f][:, :, cols].rearrange("p t (c i) -> p c t i", i=4))

        def quantise_loadings(n, f):
            quantise(ld_codes[n, f], ld_sc[n, f], ld_grouped[n, f], E4M3)

        def quantise_chance(h, n):
            quantise(ch_codes[h, n], ch_sc[h, n], ch_grouped[h, n], E5M2)

        def second_pass(acc, mt, f, n):
            h, cols = mt // 4, slice((mt % 4) * P, (mt % 4 + 1) * P)
            nc.tensor.matmul_mx(out=acc[:], lhsT=ch_codes[h, n][:, cols].bitcast(E5M2), lhsT_scale=ch_sc[h, n][:, cols],
                                rhs=ld_codes[n, f][:].bitcast(E4M3), rhs_scale=ld_sc[n, f][:], start=(n == 0), stop=(n == 3))

        def finish(mt, f, pieces=1):
            result = stage.tile([P, W], F32, name="result", bufs=6)
            width = W // pieces
            for c in range(0, W, width):
                nc.vector.tensor_tensor(out=result[:, c:c + width], in0=sums[mt][:, c:c + width],
                                        in1=base_rows[:, f * W + c:f * W + c + width], op=ALU.add)
                nc.sync.dma_start(out=out[mt * P:(mt + 1) * P, f * W + c:f * W + c + width], in_=result[:, c:c + width])

        density = {}
        turned = {}
        sums = {}

        def quantise_rca(h, g):
            quantise(rca_codes[h, g], rca_sc[h, g], rca_grouped[h, g], E4M3)

        def near(step, slots=range(4)):
            h, n = divmod(step, 4)
            if slots[0] == 0:
                density[step] = stage.tile([P, 4, W], F32, name="density", align_bytes=256)
            if step == 0:
                accs = [bank(t) for t in range(4)]
                for t in range(4):
                    first_pass(accs[t], h, n, t, 0)
                for t in range(4):
                    first_pass(accs[t], h, n, t, 1)
                    divide(density[step], accs[t], n, t)
            else:
                for t in slots:
                    acc = bank(t)
                    first_pass(acc, h, n, t, 0)
                    first_pass(acc, h, n, t, 1)
                    divide(density[step], acc, n, t)

        def turn(step):
            h, n = divmod(step, 4)
            turned[step] = [turn_openness(h, n, b, 4 + 2 * (step % 2) + b) for b in range(2)]

        def mul(step, b):
            if b == 0:
                ch_grouped[divmod(step, 4)] = stage.tile([P, W, 4], BF16, name="ch_grouped", align_bytes=256)
            multiply(ch_grouped[divmod(step, 4)], density[step], turned[step][b], b)

        def qc(step):
            quantise_chance(*divmod(step, 4))

        def second(f, first, count):
            for mt in range(first, first + count):
                sums[mt] = bank(mt)
            for n in range(4):
                for mt in range(first, first + count):
                    second_pass(sums[mt], mt, f, n)

        turn_rca(0, 0, [4, 5])
        order_codes(0, 0)
        order_scales(0)
        quantise_rca(0, 0)
        order_codes(0, 1)
        turn_rca(0, 1, [6, 7], split=True)
        quantise_rca(0, 1)
        nc.vector.reciprocal(out=inv[:], in_=tot[:])
        group_loadings(0, 0, 0)
        near(0)
        group_loadings(0, 0, 1)
        order_scales(1)
        order_both(1)
        order_scales(2)
        order_scales(3)
        turn(0)
        mul(0, 0)
        order_both(2)
        mul(0, 1)
        near(1)
        turn(1)
        group_loadings(1, 0, 0)
        mul(1, 0)
        order_both(3)
        qc(0)
        mul(1, 1)
        near(2, (0, 1))
        turn_rca(1, 0, [4, 5])
        near(2, (2, 3))
        turn(2)
        group_loadings(1, 0, 1)
        quantise_rca(1, 0)
        mul(2, 0)
        qc(1)
        mul(2, 1)
        quantise_loadings(0, 0)
        near(3, (0, 1))
        turn_rca(1, 1, [6, 7])
        near(3, (2, 3))
        turn(3)
        group_loadings(2, 0, 0)
        quantise_rca(1, 1)
        mul(3, 0)
        qc(2)
        mul(3, 1)
        near(4)
        turn(4)
        group_loadings(2, 0, 1)
        mul(4, 0)
        qc(3)
        mul(4, 1)
        quantise_loadings(1, 0)
        near(5)
        turn(5)
        group_loadings(3, 0, 0)
        mul(5, 0)
        qc(4)
        mul(5, 1)
        near(6)
        turn(6)
        group_loadings(3, 0, 1)
        mul(6, 0)
        qc(5)
        mul(6, 1)
        quantise_loadings(2, 0)
        near(7)
        turn(7)
        group_loadings(0, 1, 0)
        mul(7, 0)
        qc(6)
        quantise_loadings(3, 0)
        mul(7, 1)
        qc(7)
        group_loadings(0, 1, 1)
        second(0, 0, 5)
        quantise_loadings(0, 1)
        group_loadings(1, 1, 0)
        group_loadings(1, 1, 1)
        finish(0, 0)
        finish(1, 0)
        quantise_loadings(1, 1)
        second(0, 5, 1)
        finish(2, 0)
        finish(3, 0)
        group_loadings(2, 1, 0)
        group_loadings(2, 1, 1)
        second(0, 6, 1)
        quantise_loadings(2, 1)
        finish(4, 0)
        second(0, 7, 1)
        group_loadings(3, 1, 0)
        group_loadings(3, 1, 1)
        quantise_loadings(3, 1)
        finish(5, 0)
        finish(6, 0)
        second(1, 0, 3)
        finish(7, 0)
        finish(0, 1)
        finish(1, 1)
        finish(2, 1)
        second(1, 3, 1)
        finish(3, 1)
        second(1, 4, 1)
        finish(4, 1)
        second(1, 5, 1)
        finish(5, 1)
        second(1, 6, 1)
        finish(6, 1)
        second(1, 7, 1)
        finish(7, 1, 2)
